import numpy as np
import ml_dtypes


def mxq(x, axis, fmt="e4m3"):
    dtype, down = {"e4m3": (ml_dtypes.float8_e4m3fn, 7), "e5m2": (ml_dtypes.float8_e5m2, 14)}[fmt]
    v = np.moveaxis(np.asarray(x, np.float32).astype(ml_dtypes.bfloat16).astype(np.float64), axis, -1)
    blocks = v.reshape(v.shape[:-1] + (-1, 32))
    amax = np.abs(blocks).max(-1, keepdims=True)
    byte = np.maximum(np.where(amax > 0, np.frexp(amax)[1] - 1 + 127, 0) - down, 1)
    scale = np.exp2(byte - 127.0)
    codes = (blocks / scale).astype(np.float32).astype(dtype).astype(np.float64)
    return np.moveaxis((codes * scale).reshape(v.shape), -1, axis)


WIDE = False


def mx_kscale(k):
    if not WIDE:
        return np.ones(k)
    levels = np.array([10, -10, 5, -5, 0])
    if k % 512:
        return np.exp2(np.random.permutation(np.resize(levels, k // 32))).repeat(32)
    a = np.empty((k // 512, 16))
    for p in range(k // 512):
        a[p, :8] = np.random.permutation(np.resize(levels, 8))
        for g in range(8):
            far = levels[np.abs(levels - a[p, g]) >= 10]
            a[p, g + 8] = far[np.random.randint(len(far))]
    return np.exp2(a.ravel()).repeat(32)


BF16 = ml_dtypes.bfloat16


def bf(x):
    return np.asarray(x, np.float32).astype(BF16)


def f64(x):
    return np.asarray(x).astype(np.float64)


E2M1 = np.array([0.0, 0.5, 1.0, 1.5, 2.0, 3.0, 4.0, 6.0, -0.0, -0.5, -1.0, -1.5, -2.0, -3.0, -4.0, -6.0])


def pack_weight(w, fmt):
    k, n = w.shape
    w = f64(bf(w)).reshape(k // 32, 32, n)
    amax = np.abs(w).max(1)
    if fmt == "e4m3":
        byte = np.frexp(amax)[1] - 1 + 127 - 7
    else:
        mant, ex = np.frexp(amax / 6.0)
        byte = np.where(mant > 0.5, ex, ex - 1) + 127
    byte = np.clip(np.where(amax > 0, byte, 1), 1, 254)
    scaled = (w * np.exp2(127.0 - byte)[:, None, :]).reshape(k, n).astype(np.float32)
    by_word = np.ascontiguousarray(scaled.reshape(k // 512, 128, 4, n).transpose(0, 1, 3, 2))
    if fmt == "e4m3":
        words = by_word.astype(ml_dtypes.float8_e4m3fn).view(np.uint8)
    else:
        c = by_word.astype(ml_dtypes.float4_e2m1fn).view(np.uint8) & 0xF
        words = c[..., 0::2] | (c[..., 1::2] << 4)
    return np.ascontiguousarray(words), np.ascontiguousarray(byte.astype(np.uint8).reshape(k // 512, 16, n))


def unpack_weight(words, scales, fmt):
    g, p, n, _ = words.shape
    if fmt == "e4m3":
        vals = np.ascontiguousarray(words).view(ml_dtypes.float8_e4m3fn).astype(np.float64)
    else:
        nib = np.empty((g, p, n, 4), np.uint8)
        nib[..., 0::2] = words & 0xF
        nib[..., 1::2] = words >> 4
        vals = E2M1[nib]
    vals = vals * np.repeat(np.exp2(scales.astype(np.float64) - 127.0), 8, axis=1)[..., None]
    return vals.transpose(0, 1, 3, 2).reshape(g * 512, n)
def pack4(w):
    words, scales = pack_weight(w, "e2m1")
    return words.reshape(words.shape[0], 128, -1), scales


def unpack4(words, scales):
    return unpack_weight(words.reshape(words.shape[0], 128, -1, 2), scales, "e2m1")


def planes(Y):
    n, m = Y.shape
    b = f64(bf(Y)).reshape(n // 32, 32, m)
    amax = np.abs(b).max(1)
    byte = np.clip(np.where(amax > 0, np.frexp(amax)[1] - 1 + 127 - 7, 1), 1, 254)
    codes = (b * np.exp2(127.0 - byte)[:, None, :]).reshape(n, m).astype(np.float32).astype(ml_dtypes.float8_e4m3fn).view(np.uint8)
    words = codes.reshape(n // 512, 128, 4, m).transpose(0, 1, 3, 2)
    return np.ascontiguousarray(words), np.ascontiguousarray(byte.astype(np.uint8).reshape(n // 512, 16, m))


G, R, N, D = 4, 512, 1536, 512

def setup_inputs():
    s = mx_kscale(D)
    t = mx_kscale(N)
    img = np.random.randn(G, R, D) / np.sqrt(D)
    owner = np.stack([np.random.permutation(np.repeat(np.arange(R), N // R)) for _ in range(G)])
    match = owner[:, None, :] == np.arange(R)[None, :, None]
    spread = np.exp(0.7 * np.random.randn(D))
    spread = spread / np.sqrt(np.mean(spread ** 2))
    txt = (0.25 * img[np.arange(G)[:, None], owner] + np.random.randn(G, N, D) / np.sqrt(D)) * spread
    txt_d_words, txt_d_scales = pack4((txt.transpose(0, 2, 1) / s[:, None]).reshape(G * D, N))
    txt_n_words, txt_n_scales = pack4((txt / t[:, None]).reshape(G * N, D))
    return {
        "img": bf(img * s),
        "txt_d_words": txt_d_words, "txt_d_scales": txt_d_scales,
        "txt_n_words": txt_n_words, "txt_n_scales": txt_n_scales,
        "match": bf(match),
        "tau": bf(12.0 * np.exp(0.2 * np.random.randn(G))),
        "bias": bf(-3.0 + 0.3 * np.random.randn(G)),
        "cap_weight": bf(np.exp(0.3 * np.random.randn(G, N)) * t),
    }

def reference(img, txt_d_words, txt_d_scales, txt_n_words, txt_n_scales, match, tau, bias, cap_weight):
    A = unpack4(txt_d_words, txt_d_scales).reshape(G, D, N)
    B = unpack4(txt_n_words, txt_n_scales).reshape(G, N, D)
    tau3 = f64(tau)[:, None, None]
    logits = tau3 * (mxq(f64(img), 2) @ A) + f64(bias)[:, None, None]
    err = (1.0 / (1.0 + np.exp(-logits)) - f64(match)) * f64(cap_weight)[:, None, :]
    y = tau3 * (mxq(err, 2) @ B)
    Y = y.reshape(G * R, D).T
    words, scales = planes(Y)
    return y, words, scales

@@ -1,0 +1,373 @@
+from contextlib import ExitStack
+
+import concourse.mybir as mybir
+from concourse.masks import make_identity
+
+G, R, N, D = 4, 512, 1536, 512
+FLOPS = 2 * 2 * G * R * N * D
+
+F32 = mybir.dt.float32
+BF16 = mybir.dt.bfloat16
+I32 = mybir.dt.int32
+U32 = mybir.dt.uint32
+U8 = mybir.dt.uint8
+FP8X4 = mybir.dt.float8_e4m3fn_x4
+FP4X4 = mybir.dt.float4_e2m1fn_x4
+ACT = mybir.ActivationFunctionType
+ALU = mybir.AluOpType
+
+P = 128
+K_PASS = 512
+GROUPS = N // K_PASS
+TILES_PER_SHARD = R // P
+TILES = G * TILES_PER_SHARD
+IMG_AT = N
+Y_AT = N + D
+
+
+def tile_siglip_shard_image_grad_k7_kernel(
+    tc, img, txt_d_words, txt_d_scales, txt_n_words, txt_n_scales, match, tau, bias, cap_weight, out_0, out_1, out_2
+):
+    nc = tc.nc
+    with ExitStack() as ctx:
+        keep = ctx.enter_context(tc.tile_pool(name="keep", bufs=1))
+        work = ctx.enter_context(tc.tile_pool(name="work", bufs=3))
+        psum = ctx.enter_context(tc.psum_pool(name="psum", bufs=1))
+        ctx.enter_context(tc.manual_schedule())
+
+        ident = keep.tile([P, P], F32)
+        a_words = [keep.tile([P, 2 * N], U8, name="a_words%d" % h, align_bytes=64) for h in range(G)]
+        b_words = [keep.tile([P, GROUPS, 2 * D], U8, name="b_words%d" % h, align_bytes=64) for h in range(G)]
+        a_sc_first = keep.tile([P, 1, N], U8, align_bytes=64)
+        a_sc_rest = keep.tile([P, G - 1, N], U8, align_bytes=64)
+        b_sc_first = keep.tile([P, GROUPS, D], U8, align_bytes=64)
+        b_sc_rest = keep.tile([P, (G - 1) * GROUPS, D], U8, align_bytes=64)
+        img_sb = [keep.tile([P, TILES_PER_SHARD, D], BF16, name="img%d" % h) for h in range(G)]
+        match_sb = [keep.tile([P, N], BF16, name="match%d" % n) for n in range(TILES)]
+        y32 = [keep.tile([P, D], F32, name="y32_%d" % n) for n in range(TILES)]
+        cap_rows = keep.tile([P, K_PASS], BF16)
+        cap_t = keep.tile([P, G * GROUPS, 4], BF16)
+        tb_raw = keep.tile([P, 2, 16], BF16)
+        tb = keep.tile([P, 2, G], F32)
+        y_codes = keep.tile([P, G * R], U32, align_bytes=64)
+        y_scales = keep.tile([P, G * R], U8, align_bytes=64)
+
+        def as_words(plane):
+            return plane[:].rearrange("p a b -> p (a b)").bitcast(I32)
+
+        def load_scales(plane, src, lo, hi):
+            for q in range(4):
+                nc.sync.dma_start(
+                    out=plane[32 * q : 32 * q + 4, :, :].bitcast(I32),
+                    in_=src[lo:hi, 4 * q : 4 * q + 4, :].rearrange("c r n -> r c n").bitcast(I32),
+                )
+
+        def load_img(h, lo, hi):
+            nc.sync.dma_start(
+                out=img_sb[h][:, lo:hi, :], in_=img[h, P * lo : P * hi, :].rearrange("(c r) d -> r c d", r=P)
+            )
+
+        def load_a(h):
+            nc.sync.dma_start(out=a_words[h][:].bitcast(I32), in_=txt_d_words[h].bitcast(I32))
+
+        def load_b(h):
+            nc.sync.dma_start(
+                out=b_words[h][:].bitcast(I32),
+                in_=txt_n_words[GROUPS * h : GROUPS * (h + 1)].rearrange("g p n -> p g n").bitcast(I32),
+            )
+
+        def load_match(n):
+            h, it = divmod(n, TILES_PER_SHARD)
+            nc.sync.dma_start(out=match_sb[n][:], in_=match[h, P * it : P * (it + 1), :])
+
+        nc.vector.memset(as_words(a_sc_first), 0)
+        nc.vector.memset(as_words(b_sc_first), 0)
+        nc.vector.memset(cap_rows[:], 0.0)
+        make_identity(nc, ident[:])
+        nc.vector.memset(as_words(a_sc_rest), 0)
+        nc.vector.memset(as_words(b_sc_rest), 0)
+
+        nc.scalar.dma_start(out=tb_raw[:, 0, 0:G], in_=tau.partition_broadcast(P))
+        nc.scalar.dma_start(out=tb_raw[:, 1, 0:G], in_=bias.partition_broadcast(P))
+        load_img(0, 0, 1)
+        load_scales(a_sc_first, txt_d_scales, 0, 1)
+        load_a(0)
+        load_match(0)
+        nc.sync.dma_start(out=cap_rows[0 : G * GROUPS, :], in_=cap_weight.rearrange("h (g k) -> (h g) k", k=K_PASS))
+        load_img(0, 1, 4)
+        load_match(1)
+        load_scales(b_sc_first, txt_n_scales, 0, GROUPS)
+        load_b(0)
+        load_img(1, 0, 4)
+        load_match(2)
+        load_scales(a_sc_rest, txt_d_scales, 1, G)
+        load_scales(b_sc_rest, txt_n_scales, GROUPS, G * GROUPS)
+        load_match(3)
+        for h in range(1, G):
+            load_a(h)
+            load_match(4 * h)
+            load_b(h)
+            load_match(4 * h + 1)
+            if h + 1 < G:
+                load_img(h + 1, 0, 4)
+            load_match(4 * h + 2)
+            load_match(4 * h + 3)
+
+        def a_scale(h, g):
+            plane = a_sc_first[:, 0, :] if h == 0 else a_sc_rest[:, h - 1, :]
+            return plane[:, K_PASS * g : K_PASS * (g + 1)]
+
+        def b_scale(h, g):
+            return b_sc_first[:, g, :] if h == 0 else b_sc_rest[:, GROUPS * (h - 1) + g, :]
+
+        qin, codes, scales, s_banks, t_banks, diff, y_bank, y_bf, small = {}, {}, {}, {}, {}, {}, {}, {}, {}
+        img_mx = {}
+
+        def valid(n):
+            return 0 <= n < TILES
+
+        def stage1(n, g):
+            h = n // TILES_PER_SHARD
+            s_banks[n, g] = psum.tile([P, K_PASS], F32, name="s_bank", tag="s%d" % g)
+            nc.tensor.matmul_mx(
+                out=s_banks[n, g][:],
+                lhsT=img_mx[n][0].bitcast(FP8X4),
+                lhsT_scale=img_mx[n][1],
+                rhs=a_words[h][:, 2 * K_PASS * g : 2 * K_PASS * (g + 1)].bitcast(FP4X4),
+                rhs_scale=a_scale(h, g),
+                start=True,
+                stop=True,
+            )
+
+        def sigmoid(n, g):
+            h = n // TILES_PER_SHARD
+            if g == 0:
+                diff[n] = work.tile([P, GROUPS, 4, P], F32, name="diff")
+            nc.scalar.activation(
+                out=diff[n][:, g, :, :],
+                in_=s_banks[n, g][:].rearrange("r (p t) -> r t p", t=4),
+                func=ACT.Sigmoid,
+                bias=tb[:, 1, h : h + 1],
+                scale=tb[:, 0, h : h + 1],
+            )
+
+        def subtract(engine, n, lo, hi):
+            m = match_sb[n][:].rearrange("r (g p t) -> r g t p", g=GROUPS, t=4)
+            engine.tensor_tensor(
+                out=diff[n][:, lo:hi, :, :], in0=diff[n][:, lo:hi, :, :], in1=m[:, lo:hi, :, :], op=ALU.subtract
+            )
+
+        def turn_diff(n, g):
+            t_banks[n, g] = psum.tile([P, 4, P], F32, name="t_bank", tag="t%d" % g)
+            for t in range(4):
+                nc.tensor.transpose(t_banks[n, g][:, t, :], diff[n][:, g, t, :], ident[:])
+
+        def weigh(n, g):
+            h = n // TILES_PER_SHARD
+            nc.vector.tensor_tensor(
+                out=qin[n][:, K_PASS * g : K_PASS * (g + 1)].rearrange("p (i t) -> p i t", t=4),
+                in0=t_banks[n, g][:].rearrange("p t i -> p i t"),
+                in1=cap_t[:, GROUPS * h + g, :].unsqueeze(1).to_broadcast([P, P, 4]),
+                op=ALU.mult,
+            )
+
+        def turn_img(bank, slot, n):
+            h, it = divmod(n, TILES_PER_SHARD)
+            words = img_sb[h][:, it, :].bitcast(F32)
+            for u in range(2):
+                nc.tensor.transpose(bank[:, slot, u, :], words[:, u : 2 * P : 2], ident[:])
+
+        def turn_y(bank, slot, n):
+            words = y_bf[n][:].bitcast(F32)
+            for u in range(2):
+                nc.tensor.transpose(bank[:, slot, u, :], words[:, P * u : P * (u + 1)], ident[:])
+
+        def small_bank(tag):
+            return psum.tile([P, 2, 2, P], F32, name="small", tag=tag)
+
+        def copy_words(copy, dst, bank, lo, hi):
+            copy(
+                out=dst.bitcast(F32).rearrange("p (w r u) -> p w r u", r=P, u=2),
+                in_=bank[:, lo:hi, :, :].rearrange("p w u r -> p w r u"),
+            )
+
+        def turn_small(s):
+            small[s] = small_bank("small")
+            if valid(s + 3):
+                turn_img(small[s], 0, s + 3)
+            if valid(s - 3):
+                turn_y(small[s], 1, s - 3)
+
+        def copy_small(s):
+            lo = 0 if valid(s + 3) else 1
+            hi = 2 if valid(s - 3) else 1
+            copy_words(nc.scalar.copy, qin[s][:, IMG_AT + D * lo : IMG_AT + D * hi], small[s], lo, hi)
+
+        def new_planes(s):
+            codes[s] = work.tile([P, 4 * P], U32, name="codes", bufs=4, align_bytes=64)
+            scales[s] = work.tile([P, 4 * P], U8, name="scales", bufs=4, align_bytes=64)
+
+        def new_qin(s):
+            qin[s] = work.tile([P, N + 2 * D], BF16, name="qin", align_bytes=64)
+
+        def quantize(s, lo, hi):
+            nc.vector.quantize_mx(
+                out=codes[s][:, P * lo : P * hi].bitcast(FP8X4),
+                scales=scales[s][:, P * lo : P * hi],
+                in_=qin[s][:, K_PASS * lo : K_PASS * hi],
+            )
+
+        def slot(s, c):
+            return codes[s][:, P * c : P * (c + 1)], scales[s][:, P * c : P * (c + 1)]
+
+        def quantize_y(src, lo, hi):
+            nc.vector.quantize_mx(
+                out=y_codes[:, P * lo : P * hi].bitcast(FP8X4), scales=y_scales[:, P * lo : P * hi], in_=src
+            )
+
+        def stage2(n, tag):
+            h = n // TILES_PER_SHARD
+            y_bank[n] = psum.tile([P, D], F32, name="y_bank", tag=tag)
+            for g in range(GROUPS):
+                nc.tensor.matmul_mx(
+                    out=y_bank[n][:],
+                    lhsT=codes[n][:, P * g : P * (g + 1)].bitcast(FP8X4),
+                    lhsT_scale=scales[n][:, P * g : P * (g + 1)],
+                    rhs=b_words[h][:, g, :].bitcast(FP4X4),
+                    rhs_scale=b_scale(h, g),
+                    start=(g == 0),
+                    stop=(g == GROUPS - 1),
+                )
+
+        def store_y(n):
+            h, it = divmod(n, TILES_PER_SHARD)
+            nc.scalar.activation(out=y32[n][:], in_=y_bank[n][:], func=ACT.Copy, scale=tb[:, 0, h : h + 1])
+            nc.sync.dma_start(out=out_0[h, P * it : P * (it + 1), :], in_=y32[n][:])
+
+        def round_y(n):
+            h = n // TILES_PER_SHARD
+            y_bf[n] = work.tile([P, D], BF16, name="y_bf")
+            nc.scalar.activation(
+                out=y_bf[n][:].rearrange("r (u p e) -> r u p e", u=2, e=2),
+                in_=y_bank[n][:].rearrange("r (p u e) -> r u p e", u=2, e=2),
+                func=ACT.Copy,
+                scale=tb[:, 0, h : h + 1],
+            )
+
+        words_out = out_1[0].rearrange("p m t -> p (m t)").bitcast(I32)
+        scales_out = out_2[0].bitcast(I32)
+
+        def store_codes(lo, hi):
+            nc.sync.dma_start(out=words_out[:, P * lo : P * hi], in_=y_codes[:, P * lo : P * hi].bitcast(I32))
+
+        def store_scales(lo, hi, queues):
+            for q in range(4):
+                queues[q % len(queues)].dma_start(
+                    out=scales_out[4 * q : 4 * q + 4, P * lo // 4 : P * hi // 4],
+                    in_=y_scales[32 * q : 32 * q + 4, P * lo : P * hi].bitcast(I32),
+                )
+
+        def turn_cap():
+            bank = psum.tile([P, 4, P], F32, name="t_bank", tag="t2")
+            words = cap_rows[:].bitcast(F32)
+            for u in range(2):
+                nc.tensor.transpose(bank[:, u, :], words[:, u : 2 * P : 2], ident[:])
+            nc.vector.tensor_copy(
+                out=cap_t[:].bitcast(F32), in_=bank[:, 0:2, 0 : G * GROUPS].rearrange("p u c -> p c u")
+            )
+
+        last = TILES - 1
+
+        nc.vector.tensor_copy(out=tb[:], in_=tb_raw[:, :, 0:G])
+        bank = small_bank("small")
+        turn_img(bank, 0, 0)
+        new_qin(-1)
+        new_planes(-1)
+        copy_words(nc.vector.tensor_copy, qin[-1][:, 0:D], bank, 0, 1)
+        quantize(-1, 0, 1)
+        img_mx[0] = slot(-1, 0)
+        for g in range(GROUPS):
+            stage1(0, g)
+            sigmoid(0, g)
+        bank = small_bank("y")
+        turn_img(bank, 0, 1)
+        turn_img(bank, 1, 2)
+        copy_words(nc.vector.tensor_copy, qin[-1][:, 2 * D : 4 * D], bank, 0, 2)
+        turn_cap()
+        subtract(nc.vector, 0, 0, 1)
+        quantize(-1, 2, 4)
+        img_mx[1] = slot(-1, 2)
+        img_mx[2] = slot(-1, 3)
+        subtract(nc.vector, 0, 1, 2)
+        subtract(nc.gpsimd, 0, 2, 3)
+        for g in range(GROUPS):
+            turn_diff(0, g)
+            stage1(1, g)
+            sigmoid(1, g)
+        subtract(nc.gpsimd, 1, 2, 3)
+
+        for s in range(TILES):
+            if s >= 1 and valid(s + 1):
+                for g in range(GROUPS):
+                    stage1(s + 1, g)
+            if s >= 1:
+                copy_small(s - 1)
+            if s >= 1 and valid(s + 1):
+                for g in range(GROUPS):
+                    sigmoid(s + 1, g)
+                subtract(nc.gpsimd, s + 1, 2, 3)
+            if valid(s - 2):
+                stage2(s - 2, "y")
+                store_y(s - 2)
+                round_y(s - 2)
+            if s >= 1:
+                subtract(nc.vector, s, 0, 2)
+                new_planes(s - 1)
+                if valid(s + 2):
+                    quantize(s - 1, 0, 4)
+                    img_mx[s + 2] = slot(s - 1, 3)
+                else:
+                    quantize(s - 1, 0, 2)
+                    quantize(s - 1, 2, 3)
+            if valid(s - 4):
+                quantize_y(qin[s - 1][:, Y_AT : Y_AT + D], s - 4, s - 3)
+                if s % TILES_PER_SHARD == 3:
+                    store_codes(s - 7, s - 3)
+            if s >= 1:
+                for g in range(GROUPS):
+                    turn_diff(s, g)
+            turn_small(s)
+            new_qin(s)
+            if s < last:
+                for g in range(GROUPS):
+                    weigh(s, g)
+        store_scales(0, last - 3, [nc.sync])
+
+        copy_small(last)
+        stage2(last - 1, "y")
+        round_y(last - 1)
+        store_y(last - 1)
+        new_planes(last)
+        weigh(last, 0)
+        weigh(last, 1)
+        quantize(last, 0, 1)
+        weigh(last, 2)
+        quantize(last, 1, 2)
+        quantize(last, 2, 3)
+        quantize_y(qin[last][:, Y_AT : Y_AT + D], last - 3, last - 2)
+        bank = small_bank("s1")
+        turn_y(bank, 0, last - 2)
+        turn_y(bank, 1, last - 1)
+        stage2(last, "s0")
+        new_qin(last + 1)
+        copy_words(nc.vector.tensor_copy, qin[last + 1][:, 0 : 2 * D], bank, 0, 2)
+        round_y(last)
+        store_y(last)
+        quantize_y(qin[last + 1][:, 0 : 2 * D], last - 2, last)
+        store_codes(last - 3, last)
+        bank = small_bank("s2")
+        turn_y(bank, 0, last)
+        copy_words(nc.vector.tensor_copy, qin[last + 1][:, 2 * D : 3 * D], bank, 0, 1)
+        quantize_y(qin[last + 1][:, 2 * D : 3 * D], last, last + 1)
+        store_codes(last, last + 1)
+        store_scales(last - 3, last + 1, [nc.scalar, nc.sync])

@@ -21,6 +21,7 @@ K_PASS = 512
 GROUPS = N // K_PASS
 TILES_PER_SHARD = R // P
 TILES = G * TILES_PER_SHARD
+S_TAGS = ("s0", "s1", "s2")
 IMG_AT = N
 Y_AT = N + D
 
@@ -43,7 +44,7 @@ def tile_siglip_shard_image_grad_k7_kernel(
         b_sc_first = keep.tile([P, GROUPS, D], U8, align_bytes=64)
         b_sc_rest = keep.tile([P, (G - 1) * GROUPS, D], U8, align_bytes=64)
         img_sb = [keep.tile([P, TILES_PER_SHARD, D], BF16, name="img%d" % h) for h in range(G)]
-        match_sb = [keep.tile([P, N], BF16, name="match%d" % n) for n in range(TILES)]
+        match_sb = [keep.tile([P, TILES_PER_SHARD, N], BF16, name="match%d" % h) for h in range(G)]
         y32 = [keep.tile([P, D], F32, name="y32_%d" % n) for n in range(TILES)]
         cap_rows = keep.tile([P, K_PASS], BF16)
         cap_t = keep.tile([P, G * GROUPS, 4], BF16)
@@ -76,42 +77,45 @@ def tile_siglip_shard_image_grad_k7_kernel(
                 in_=txt_n_words[GROUPS * h : GROUPS * (h + 1)].rearrange("g p n -> p g n").bitcast(I32),
             )
 
-        def load_match(n):
+        def load_match(h, lo, hi):
+            nc.sync.dma_start(
+                out=match_sb[h][:, lo:hi, :], in_=match[h, P * lo : P * hi, :].rearrange("(c r) n -> r c n", r=P)
+            )
+
+        def match_tile(n):
             h, it = divmod(n, TILES_PER_SHARD)
-            nc.sync.dma_start(out=match_sb[n][:], in_=match[h, P * it : P * (it + 1), :])
+            return match_sb[h][:, it, :]
 
         nc.vector.memset(as_words(a_sc_first), 0)
         nc.vector.memset(as_words(b_sc_first), 0)
         nc.vector.memset(cap_rows[:], 0.0)
         make_identity(nc, ident[:])
-        nc.vector.memset(as_words(a_sc_rest), 0)
-        nc.vector.memset(as_words(b_sc_rest), 0)
 
         nc.scalar.dma_start(out=tb_raw[:, 0, 0:G], in_=tau.partition_broadcast(P))
         nc.scalar.dma_start(out=tb_raw[:, 1, 0:G], in_=bias.partition_broadcast(P))
-        load_img(0, 0, 1)
-        load_scales(a_sc_first, txt_d_scales, 0, 1)
+        load_img(0, 0, 2)
         load_a(0)
-        load_match(0)
+        load_scales(a_sc_first, txt_d_scales, 0, 1)
+        load_match(0, 0, 1)
+        load_img(0, 2, 4)
         nc.sync.dma_start(out=cap_rows[0 : G * GROUPS, :], in_=cap_weight.rearrange("h (g k) -> (h g) k", k=K_PASS))
-        load_img(0, 1, 4)
-        load_match(1)
+        load_match(0, 1, 2)
+        load_img(1, 0, 4)
+        load_match(0, 2, 3)
         load_scales(b_sc_first, txt_n_scales, 0, GROUPS)
         load_b(0)
-        load_img(1, 0, 4)
-        load_match(2)
-        load_scales(a_sc_rest, txt_d_scales, 1, G)
-        load_scales(b_sc_rest, txt_n_scales, GROUPS, G * GROUPS)
-        load_match(3)
-        for h in range(1, G):
-            load_a(h)
-            load_match(4 * h)
-            load_b(h)
-            load_match(4 * h + 1)
-            if h + 1 < G:
-                load_img(h + 1, 0, 4)
-            load_match(4 * h + 2)
-            load_match(4 * h + 3)
+        load_match(0, 3, 4)
+
+        def load_later_shards():
+            load_scales(a_sc_rest, txt_d_scales, 1, G)
+            load_scales(b_sc_rest, txt_n_scales, GROUPS, G * GROUPS)
+            for h in range(1, G):
+                load_a(h)
+                load_match(h, 0, 2)
+                load_b(h)
+                if h + 1 < G:
+                    load_img(h + 1, 0, 4)
+                load_match(h, 2, 4)
 
         def a_scale(h, g):
             plane = a_sc_first[:, 0, :] if h == 0 else a_sc_rest[:, h - 1, :]
@@ -121,14 +125,16 @@ def tile_siglip_shard_image_grad_k7_kernel(
             return b_sc_first[:, g, :] if h == 0 else b_sc_rest[:, GROUPS * (h - 1) + g, :]
 
         qin, codes, scales, s_banks, t_banks, diff, y_bank, y_bf, small = {}, {}, {}, {}, {}, {}, {}, {}, {}
-        img_mx = {}
+        img_mx, sig_pool, diff_pool, s_tags, t_tags = {}, {}, {}, {}, {}
+        free_s, free_t = list(S_TAGS), ["t0", "t1", "t2"]
 
         def valid(n):
             return 0 <= n < TILES
 
-        def stage1(n, g):
+        def stage1(n, g, spare=None):
             h = n // TILES_PER_SHARD
-            s_banks[n, g] = psum.tile([P, K_PASS], F32, name="s_bank", tag="s%d" % g)
+            s_tags[n, g] = spare or free_s.pop(0)
+            s_banks[n, g] = psum.tile([P, K_PASS], F32, name="s_bank", tag=s_tags[n, g])
             nc.tensor.matmul_mx(
                 out=s_banks[n, g][:],
                 lhsT=img_mx[n][0].bitcast(FP8X4),
@@ -139,30 +145,45 @@ def tile_siglip_shard_image_grad_k7_kernel(
                 stop=True,
             )
 
+        def local(ap):
+            return ap.rearrange("r t (q c) -> r q t c", c=4)
+
         def sigmoid(n, g):
             h = n // TILES_PER_SHARD
-            if g == 0:
-                diff[n] = work.tile([P, GROUPS, 4, P], F32, name="diff")
+            if s_tags[n, g] in S_TAGS:
+                free_s.append(s_tags[n, g])
+            if n not in diff:
+                diff[n] = work.tile([P, 4, 2 * P], F32, name="diff")
+                sig_pool[n] = work.tile([P, 4, P], F32, name="sig_pool")
+            dst = diff[n][:, :, P * g : P * (g + 1)] if g < 2 else sig_pool[n][:]
             nc.scalar.activation(
-                out=diff[n][:, g, :, :],
-                in_=s_banks[n, g][:].rearrange("r (p t) -> r t p", t=4),
+                out=local(dst),
+                in_=s_banks[n, g][:].rearrange("r (q c t) -> r q t c", c=4, t=4),
                 func=ACT.Sigmoid,
                 bias=tb[:, 1, h : h + 1],
                 scale=tb[:, 0, h : h + 1],
             )
 
-        def subtract(engine, n, lo, hi):
-            m = match_sb[n][:].rearrange("r (g p t) -> r g t p", g=GROUPS, t=4)
-            engine.tensor_tensor(
-                out=diff[n][:, lo:hi, :, :], in0=diff[n][:, lo:hi, :, :], in1=m[:, lo:hi, :, :], op=ALU.subtract
-            )
+        def subtract(n, lo, hi):
+            part = local(diff[n][:, :, P * lo : P * hi])
+            m = match_tile(n)[:, K_PASS * lo : K_PASS * hi].rearrange("r (q c t) -> r q t c", c=4, t=4)
+            nc.vector.tensor_tensor(out=part, in0=part, in1=m, op=ALU.subtract)
+
+        def subtract_pool(engine, n):
+            host = sig_pool[n][:].rearrange("r t p -> r (t p)").bitcast(BF16) if n == 0 else match_tile(n)
+            diff_pool[n] = host[:, 0 : 2 * K_PASS].bitcast(F32).rearrange("r (t p) -> r t p", t=4)
+            m = match_tile(n)[:, 2 * K_PASS : 3 * K_PASS].rearrange("r (p t) -> r t p", t=4)
+            engine.tensor_tensor(out=diff_pool[n], in0=sig_pool[n][:], in1=m, op=ALU.subtract)
 
         def turn_diff(n, g):
-            t_banks[n, g] = psum.tile([P, 4, P], F32, name="t_bank", tag="t%d" % g)
+            t_tags[n, g] = free_t.pop(0)
+            t_banks[n, g] = psum.tile([P, 4, P], F32, name="t_bank", tag=t_tags[n, g])
             for t in range(4):
-                nc.tensor.transpose(t_banks[n, g][:, t, :], diff[n][:, g, t, :], ident[:])
+                src = diff[n][:, t, P * g : P * (g + 1)] if g < 2 else diff_pool[n][:, t, :]
+                nc.tensor.transpose(t_banks[n, g][:, t, :], src, ident[:])
 
         def weigh(n, g):
+            free_t.append(t_tags[n, g])
             h = n // TILES_PER_SHARD
             nc.vector.tensor_tensor(
                 out=qin[n][:, K_PASS * g : K_PASS * (g + 1)].rearrange("p (i t) -> p i t", t=4),
@@ -193,22 +214,22 @@ def tile_siglip_shard_image_grad_k7_kernel(
 
         def turn_small(s):
             small[s] = small_bank("small")
-            if valid(s + 3):
-                turn_img(small[s], 0, s + 3)
+            if valid(s + 5):
+                turn_img(small[s], 0, s + 5)
             if valid(s - 3):
                 turn_y(small[s], 1, s - 3)
 
         def copy_small(s):
-            lo = 0 if valid(s + 3) else 1
+            lo = 0 if valid(s + 5) else 1
             hi = 2 if valid(s - 3) else 1
-            copy_words(nc.scalar.copy, qin[s][:, IMG_AT + D * lo : IMG_AT + D * hi], small[s], lo, hi)
+            copy_words(nc.scalar.copy, qin[s + 1][:, IMG_AT + D * lo : IMG_AT + D * hi], small[s], lo, hi)
 
         def new_planes(s):
             codes[s] = work.tile([P, 4 * P], U32, name="codes", bufs=4, align_bytes=64)
             scales[s] = work.tile([P, 4 * P], U8, name="scales", bufs=4, align_bytes=64)
 
         def new_qin(s):
-            qin[s] = work.tile([P, N + 2 * D], BF16, name="qin", align_bytes=64)
+            qin[s] = work.tile([P, N + 2 * D], BF16, name="qin", bufs=5, align_bytes=64)
 
         def quantize(s, lo, hi):
             nc.vector.quantize_mx(
@@ -225,18 +246,18 @@ def tile_siglip_shard_image_grad_k7_kernel(
                 out=y_codes[:, P * lo : P * hi].bitcast(FP8X4), scales=y_scales[:, P * lo : P * hi], in_=src
             )
 
-        def stage2(n, tag):
+        def stage2(n, tag, order=(0, 1, 2)):
             h = n // TILES_PER_SHARD
             y_bank[n] = psum.tile([P, D], F32, name="y_bank", tag=tag)
-            for g in range(GROUPS):
+            for g in order:
                 nc.tensor.matmul_mx(
                     out=y_bank[n][:],
                     lhsT=codes[n][:, P * g : P * (g + 1)].bitcast(FP8X4),
                     lhsT_scale=scales[n][:, P * g : P * (g + 1)],
                     rhs=b_words[h][:, g, :].bitcast(FP4X4),
                     rhs_scale=b_scale(h, g),
-                    start=(g == 0),
-                    stop=(g == GROUPS - 1),
+                    start=(g == order[0]),
+                    stop=(g == order[-1]),
                 )
 
         def store_y(n):
@@ -268,7 +289,7 @@ def tile_siglip_shard_image_grad_k7_kernel(
                 )
 
         def turn_cap():
-            bank = psum.tile([P, 4, P], F32, name="t_bank", tag="t2")
+            bank = psum.tile([P, 4, P], F32, name="t_bank", tag="t1")
             words = cap_rows[:].bitcast(F32)
             for u in range(2):
                 nc.tensor.transpose(bank[:, u, :], words[:, u : 2 * P : 2], ident[:])
@@ -279,95 +300,119 @@ def tile_siglip_shard_image_grad_k7_kernel(
         last = TILES - 1
 
         nc.vector.tensor_copy(out=tb[:], in_=tb_raw[:, :, 0:G])
-        bank = small_bank("small")
-        turn_img(bank, 0, 0)
         new_qin(-1)
         new_planes(-1)
-        copy_words(nc.vector.tensor_copy, qin[-1][:, 0:D], bank, 0, 1)
+        for n in range(TILES_PER_SHARD):
+            img_mx[n] = slot(-1, n)
+        banks = [small_bank("t0"), small_bank("t1")]
+        for n in range(2):
+            turn_img(banks[n], 0, n)
+        copy_words(nc.vector.tensor_copy, qin[-1][:, 0:D], banks[0], 0, 1)
         quantize(-1, 0, 1)
-        img_mx[0] = slot(-1, 0)
+        copy_words(nc.vector.tensor_copy, qin[-1][:, D : 2 * D], banks[1], 0, 1)
+        nc.vector.memset(as_words(a_sc_rest), 0)
+        quantize(-1, 1, 2)
         for g in range(GROUPS):
             stage1(0, g)
             sigmoid(0, g)
-        bank = small_bank("y")
-        turn_img(bank, 0, 1)
-        turn_img(bank, 1, 2)
-        copy_words(nc.vector.tensor_copy, qin[-1][:, 2 * D : 4 * D], bank, 0, 2)
         turn_cap()
-        subtract(nc.vector, 0, 0, 1)
+        bank = small_bank("t2")
+        turn_img(bank, 0, 2)
+        turn_img(bank, 1, 3)
+        stage1(1, 0, "y")
+        stage1(1, 1, "small")
+        stage1(1, 2)
+        for g in range(GROUPS):
+            sigmoid(1, g)
+        subtract(0, 0, 1)
+        subtract(0, 1, 2)
+        copy_words(nc.vector.tensor_copy, qin[-1][:, 2 * D : 4 * D], bank, 0, 2)
+        subtract_pool(nc.vector, 0)
         quantize(-1, 2, 4)
-        img_mx[1] = slot(-1, 2)
-        img_mx[2] = slot(-1, 3)
-        subtract(nc.vector, 0, 1, 2)
-        subtract(nc.gpsimd, 0, 2, 3)
+        subtract(1, 0, 2)
+        nc.gpsimd.memset(as_words(b_sc_rest), 0)
+        load_later_shards()
         for g in range(GROUPS):
             turn_diff(0, g)
-            stage1(1, g)
-            sigmoid(1, g)
-        subtract(nc.gpsimd, 1, 2, 3)
+        turn_small(-1)
+        new_qin(0)
+        copy_small(-1)
 
-        for s in range(TILES):
-            if s >= 1 and valid(s + 1):
-                for g in range(GROUPS):
-                    stage1(s + 1, g)
-            if s >= 1:
-                copy_small(s - 1)
-            if s >= 1 and valid(s + 1):
-                for g in range(GROUPS):
-                    sigmoid(s + 1, g)
-                subtract(nc.gpsimd, s + 1, 2, 3)
+        def quantize_step(s):
+            new_planes(s)
+            if valid(s + 4):
+                quantize(s, 0, 4)
+                img_mx[s + 4] = slot(s, 3)
+            else:
+                quantize(s, 0, 2)
+                quantize(s, 2, 3)
+
+        def quantize_step_y(s):
+            quantize_y(qin[s][:, Y_AT : Y_AT + D], s - 4, s - 3)
+
+        for s in range(last):
+            subtract_pool(nc.gpsimd, s + 1)
+            if valid(s + 2):
+                for g in (2, 0, 1):
+                    stage1(s + 2, g)
+                for g in (1, 0, 2):
+                    sigmoid(s + 2, g)
+            for g in (2, 0, 1):
+                weigh(s, g)
             if valid(s - 2):
                 stage2(s - 2, "y")
                 store_y(s - 2)
                 round_y(s - 2)
-            if s >= 1:
-                subtract(nc.vector, s, 0, 2)
-                new_planes(s - 1)
-                if valid(s + 2):
-                    quantize(s - 1, 0, 4)
-                    img_mx[s + 2] = slot(s - 1, 3)
-                else:
-                    quantize(s - 1, 0, 2)
-                    quantize(s - 1, 2, 3)
-            if valid(s - 4):
-                quantize_y(qin[s - 1][:, Y_AT : Y_AT + D], s - 4, s - 3)
-                if s % TILES_PER_SHARD == 3:
-                    store_codes(s - 7, s - 3)
-            if s >= 1:
-                for g in range(GROUPS):
-                    turn_diff(s, g)
             turn_small(s)
-            new_qin(s)
-            if s < last:
-                for g in range(GROUPS):
-                    weigh(s, g)
-        store_scales(0, last - 3, [nc.sync])
+            for g in range(GROUPS):
+                turn_diff(s + 1, g)
+            if s >= 1:
+                quantize_step(s - 1)
+            if valid(s - 5) and s < last - 1:
+                quantize_step_y(s - 1)
+                if s % TILES_PER_SHARD == 0:
+                    store_codes(s - 8, s - 4)
+                if s == last - 3:
+                    store_scales(0, s - 4, [nc.sync])
+            if valid(s + 2):
+                subtract(s + 2, 0, 2)
+            new_qin(s + 1)
+            copy_small(s)
 
-        copy_small(last)
+        quantize_step(last - 1)
+        stage2(last - 2, "s0")
+        round_y(last - 2)
+        store_y(last - 2)
         stage2(last - 1, "y")
+        pair = small_bank("s1")
+        turn_y(pair, 0, last - 3)
+        turn_y(pair, 1, last - 2)
         round_y(last - 1)
         store_y(last - 1)
         new_planes(last)
+        weigh(last, 2)
         weigh(last, 0)
+        quantize(last, 2, 3)
         weigh(last, 1)
         quantize(last, 0, 1)
-        weigh(last, 2)
         quantize(last, 1, 2)
-        quantize(last, 2, 3)
-        quantize_y(qin[last][:, Y_AT : Y_AT + D], last - 3, last - 2)
-        bank = small_bank("s1")
-        turn_y(bank, 0, last - 2)
-        turn_y(bank, 1, last - 1)
-        stage2(last, "s0")
-        new_qin(last + 1)
-        copy_words(nc.vector.tensor_copy, qin[last + 1][:, 0 : 2 * D], bank, 0, 2)
+        stage2(last, "s2", (2, 0, 1))
         round_y(last)
+        new_qin(last + 1)
+        rest = qin[last + 1]
+        copy_words(nc.vector.tensor_copy, rest[:, 0 : 2 * D], pair, 0, 2)
+        for s in range(last - 2, last + 1):
+            quantize_step_y(s)
+        store_codes(last - 7, last - 3)
         store_y(last)
-        quantize_y(qin[last + 1][:, 0 : 2 * D], last - 2, last)
-        store_codes(last - 3, last)
-        bank = small_bank("s2")
+        bank = small_bank("small")
+        turn_y(bank, 0, last - 1)
+        copy_words(nc.vector.tensor_copy, rest[:, 2 * D : 3 * D], bank, 0, 1)
+        quantize_y(rest[:, 0 : 2 * D], last - 3, last - 1)
+        quantize_y(rest[:, 2 * D : 3 * D], last - 1, last)
+        bank = small_bank("s0")
         turn_y(bank, 0, last)
-        copy_words(nc.vector.tensor_copy, qin[last + 1][:, 2 * D : 3 * D], bank, 0, 1)
-        quantize_y(qin[last + 1][:, 2 * D : 3 * D], last, last + 1)
-        store_codes(last, last + 1)
-        store_scales(last - 3, last + 1, [nc.scalar, nc.sync])
+        copy_words(nc.vector.tensor_copy, rest[:, 3 * D : 4 * D], bank, 0, 1)
+        quantize_y(rest[:, 3 * D : 4 * D], last, last + 1)
+        store_codes(last - 3, last + 1)
+        store_scales(last - 7, last + 1, [nc.scalar, nc.sync])

@@ -48,7 +48,7 @@ def tile_siglip_shard_image_grad_k7_kernel(
         y32 = [keep.tile([P, D], F32, name="y32_%d" % n) for n in range(TILES)]
         cap_rows = keep.tile([P, K_PASS], BF16)
         cap_t = keep.tile([P, G * GROUPS, 4], BF16)
-        tb_raw = keep.tile([P, 2, 16], BF16)
+        tb_col = keep.tile([P, 2], BF16)
         tb = keep.tile([P, 2, G], F32)
         y_codes = keep.tile([P, G * R], U32, align_bytes=64)
         y_scales = keep.tile([P, G * R], U8, align_bytes=64)
@@ -86,19 +86,20 @@ def tile_siglip_shard_image_grad_k7_kernel(
             h, it = divmod(n, TILES_PER_SHARD)
             return match_sb[h][:, it, :]
 
+        nc.vector.memset(tb_col[:], 0.0)
         nc.vector.memset(as_words(a_sc_first), 0)
         nc.vector.memset(as_words(b_sc_first), 0)
         nc.vector.memset(cap_rows[:], 0.0)
         make_identity(nc, ident[:])
 
-        nc.scalar.dma_start(out=tb_raw[:, 0, 0:G], in_=tau.partition_broadcast(P))
-        nc.scalar.dma_start(out=tb_raw[:, 1, 0:G], in_=bias.partition_broadcast(P))
+        nc.scalar.dma_start(out=tb_col[0:2, :], in_=tau.rearrange("(r e) -> r e", e=2))
+        nc.scalar.dma_start(out=tb_col[2:4, :], in_=bias.rearrange("(r e) -> r e", e=2))
         load_img(0, 0, 2)
         load_a(0)
         load_scales(a_sc_first, txt_d_scales, 0, 1)
         load_match(0, 0, 1)
-        load_img(0, 2, 4)
         nc.sync.dma_start(out=cap_rows[0 : G * GROUPS, :], in_=cap_weight.rearrange("h (g k) -> (h g) k", k=K_PASS))
+        load_img(0, 2, 4)
         load_match(0, 1, 2)
         load_img(1, 0, 4)
         load_match(0, 2, 3)
@@ -108,14 +109,15 @@ def tile_siglip_shard_image_grad_k7_kernel(
 
         def load_later_shards():
             load_scales(a_sc_rest, txt_d_scales, 1, G)
-            load_scales(b_sc_rest, txt_n_scales, GROUPS, G * GROUPS)
             for h in range(1, G):
                 load_a(h)
                 load_match(h, 0, 2)
-                load_b(h)
                 if h + 1 < G:
                     load_img(h + 1, 0, 4)
+                if h == 1:
+                    load_scales(b_sc_rest, txt_n_scales, GROUPS, G * GROUPS)
                 load_match(h, 2, 4)
+                load_b(h)
 
         def a_scale(h, g):
             plane = a_sc_first[:, 0, :] if h == 0 else a_sc_rest[:, h - 1, :]
@@ -214,13 +216,13 @@ def tile_siglip_shard_image_grad_k7_kernel(
 
         def turn_small(s):
             small[s] = small_bank("small")
-            if valid(s + 5):
-                turn_img(small[s], 0, s + 5)
+            if valid(s + 6):
+                turn_img(small[s], 0, s + 6)
             if valid(s - 3):
                 turn_y(small[s], 1, s - 3)
 
         def copy_small(s):
-            lo = 0 if valid(s + 5) else 1
+            lo = 0 if valid(s + 6) else 1
             hi = 2 if valid(s - 3) else 1
             copy_words(nc.scalar.copy, qin[s + 1][:, IMG_AT + D * lo : IMG_AT + D * hi], small[s], lo, hi)
 
@@ -293,13 +295,15 @@ def tile_siglip_shard_image_grad_k7_kernel(
             words = cap_rows[:].bitcast(F32)
             for u in range(2):
                 nc.tensor.transpose(bank[:, u, :], words[:, u : 2 * P : 2], ident[:])
+            return bank
+
+        def copy_cap(bank):
             nc.vector.tensor_copy(
                 out=cap_t[:].bitcast(F32), in_=bank[:, 0:2, 0 : G * GROUPS].rearrange("p u c -> p c u")
             )
 
         last = TILES - 1
 
-        nc.vector.tensor_copy(out=tb[:], in_=tb_raw[:, :, 0:G])
         new_qin(-1)
         new_planes(-1)
         for n in range(TILES_PER_SHARD):
@@ -310,17 +314,20 @@ def tile_siglip_shard_image_grad_k7_kernel(
         copy_words(nc.vector.tensor_copy, qin[-1][:, 0:D], banks[0], 0, 1)
         quantize(-1, 0, 1)
         copy_words(nc.vector.tensor_copy, qin[-1][:, D : 2 * D], banks[1], 0, 1)
+        spread = psum.tile([P, P], F32, name="spread", tag="small")
+        nc.tensor.transpose(spread[:], tb_col[:].bitcast(F32).to_broadcast([P, P]), ident[:])
+        nc.vector.tensor_copy(out=tb[:].rearrange("p a h -> p (a h)"), in_=spread[:, 0:G].bitcast(BF16))
         nc.vector.memset(as_words(a_sc_rest), 0)
         quantize(-1, 1, 2)
         for g in range(GROUPS):
             stage1(0, g)
             sigmoid(0, g)
-        turn_cap()
         bank = small_bank("t2")
         turn_img(bank, 0, 2)
         turn_img(bank, 1, 3)
         stage1(1, 0, "y")
         stage1(1, 1, "small")
+        cap_bank = turn_cap()
         stage1(1, 2)
         for g in range(GROUPS):
             sigmoid(1, g)
@@ -328,23 +335,25 @@ def tile_siglip_shard_image_grad_k7_kernel(
         subtract(0, 1, 2)
         copy_words(nc.vector.tensor_copy, qin[-1][:, 2 * D : 4 * D], bank, 0, 2)
         subtract_pool(nc.vector, 0)
+        copy_cap(cap_bank)
         quantize(-1, 2, 4)
         subtract(1, 0, 2)
         nc.gpsimd.memset(as_words(b_sc_rest), 0)
         load_later_shards()
         for g in range(GROUPS):
             turn_diff(0, g)
-        turn_small(-1)
         new_qin(0)
-        copy_small(-1)
 
-        def quantize_step(s):
+        def quantize_early(s):
             new_planes(s)
-            if valid(s + 4):
-                quantize(s, 0, 4)
-                img_mx[s + 4] = slot(s, 3)
-            else:
+            if not valid(s + 5):
                 quantize(s, 0, 2)
+
+        def quantize_late(s):
+            if valid(s + 5):
+                quantize(s, 0, 4)
+                img_mx[s + 5] = slot(s, 3)
+            else:
                 quantize(s, 2, 3)
 
         def quantize_step_y(s):
@@ -353,10 +362,16 @@ def tile_siglip_shard_image_grad_k7_kernel(
         for s in range(last):
             subtract_pool(nc.gpsimd, s + 1)
             if valid(s + 2):
-                for g in (2, 0, 1):
-                    stage1(s + 2, g)
                 for g in (1, 0, 2):
+                    stage1(s + 2, g)
+                for g in range(GROUPS):
                     sigmoid(s + 2, g)
+            if s == 0:
+                bank = small_bank("y")
+                turn_img(bank, 0, 4)
+                turn_img(bank, 1, 5)
+                copy_words(nc.scalar.copy, qin[-1][:, Y_AT : Y_AT + D], bank, 0, 1)
+                copy_words(nc.scalar.copy, qin[0][:, IMG_AT : IMG_AT + D], bank, 1, 2)
             for g in (2, 0, 1):
                 weigh(s, g)
             if valid(s - 2):
@@ -366,20 +381,29 @@ def tile_siglip_shard_image_grad_k7_kernel(
             turn_small(s)
             for g in range(GROUPS):
                 turn_diff(s + 1, g)
-            if s >= 1:
-                quantize_step(s - 1)
             if valid(s - 5) and s < last - 1:
                 quantize_step_y(s - 1)
                 if s % TILES_PER_SHARD == 0:
                     store_codes(s - 8, s - 4)
                 if s == last - 3:
                     store_scales(0, s - 4, [nc.sync])
+            if s >= 1:
+                quantize_early(s - 1)
             if valid(s + 2):
                 subtract(s + 2, 0, 2)
+            if s >= 1:
+                quantize_late(s - 1)
+            else:
+                new_planes(-2)
+                img_mx[4] = slot(-2, 0)
+                nc.vector.quantize_mx(
+                    out=img_mx[4][0].bitcast(FP8X4), scales=img_mx[4][1], in_=qin[-1][:, Y_AT : Y_AT + D]
+                )
             new_qin(s + 1)
             copy_small(s)
 
-        quantize_step(last - 1)
+        quantize_early(last - 1)
+        quantize_late(last - 1)
         stage2(last - 2, "s0")
         round_y(last - 2)
         store_y(last - 2)

from contextlib import ExitStack

import concourse.mybir as mybir
from concourse.masks import make_identity

G, R, N, D = 4, 512, 1536, 512
FLOPS = 2 * 2 * G * R * N * D

F32 = mybir.dt.float32
BF16 = mybir.dt.bfloat16
I32 = mybir.dt.int32
U32 = mybir.dt.uint32
U8 = mybir.dt.uint8
FP8X4 = mybir.dt.float8_e4m3fn_x4
FP4X4 = mybir.dt.float4_e2m1fn_x4
ACT = mybir.ActivationFunctionType
ALU = mybir.AluOpType

P = 128
K_PASS = 512
GROUPS = N // K_PASS
TILES_PER_SHARD = R // P
TILES = G * TILES_PER_SHARD
S_TAGS = ("s0", "s1", "s2")
IMG_AT = N
Y_AT = N + D


def tile_siglip_shard_image_grad_k7_kernel(
    tc, img, txt_d_words, txt_d_scales, txt_n_words, txt_n_scales, match, tau, bias, cap_weight, out_0, out_1, out_2
):
    nc = tc.nc
    with ExitStack() as ctx:
        keep = ctx.enter_context(tc.tile_pool(name="keep", bufs=1))
        work = ctx.enter_context(tc.tile_pool(name="work", bufs=3))
        psum = ctx.enter_context(tc.psum_pool(name="psum", bufs=1))
        ctx.enter_context(tc.manual_schedule())

        ident = keep.tile([P, P], F32)
        a_words = [keep.tile([P, 2 * N], U8, name="a_words%d" % h, align_bytes=64) for h in range(G)]
        b_words = [keep.tile([P, GROUPS, 2 * D], U8, name="b_words%d" % h, align_bytes=64) for h in range(G)]
        a_sc_first = keep.tile([P, 1, N], U8, align_bytes=64)
        a_sc_rest = keep.tile([P, G - 1, N], U8, align_bytes=64)
        b_sc_first = keep.tile([P, GROUPS, D], U8, align_bytes=64)
        b_sc_rest = keep.tile([P, (G - 1) * GROUPS, D], U8, align_bytes=64)
        img_sb = [keep.tile([P, TILES_PER_SHARD, D], BF16, name="img%d" % h) for h in range(G)]
        match_sb = [keep.tile([P, TILES_PER_SHARD, N], BF16, name="match%d" % h) for h in range(G)]
        y32 = [keep.tile([P, D], F32, name="y32_%d" % n) for n in range(TILES)]
        cap_rows = keep.tile([P, K_PASS], BF16)
        cap_t = keep.tile([P, G * GROUPS, 4], BF16)
        tb_col = keep.tile([P, 2], BF16)
        tb = keep.tile([P, 2, G], F32)
        y_codes = keep.tile([P, G * R], U32, align_bytes=64)
        y_scales = keep.tile([P, G * R], U8, align_bytes=64)

        def as_words(plane):
            return plane[:].rearrange("p a b -> p (a b)").bitcast(I32)

        def load_scales(plane, src, lo, hi):
            for q in range(4):
                nc.sync.dma_start(
                    out=plane[32 * q : 32 * q + 4, :, :].bitcast(I32),
                    in_=src[lo:hi, 4 * q : 4 * q + 4, :].rearrange("c r n -> r c n").bitcast(I32),
                )

        def load_img(h, lo, hi):
            nc.sync.dma_start(
                out=img_sb[h][:, lo:hi, :], in_=img[h, P * lo : P * hi, :].rearrange("(c r) d -> r c d", r=P)
            )

        def load_a(h):
            nc.sync.dma_start(out=a_words[h][:].bitcast(I32), in_=txt_d_words[h].bitcast(I32))

        def load_b(h):
            nc.sync.dma_start(
                out=b_words[h][:].bitcast(I32),
                in_=txt_n_words[GROUPS * h : GROUPS * (h + 1)].rearrange("g p n -> p g n").bitcast(I32),
            )

        def load_match(h, lo, hi):
            nc.sync.dma_start(
                out=match_sb[h][:, lo:hi, :], in_=match[h, P * lo : P * hi, :].rearrange("(c r) n -> r c n", r=P)
            )

        def match_tile(n):
            h, it = divmod(n, TILES_PER_SHARD)
            return match_sb[h][:, it, :]

        nc.vector.memset(tb_col[:], 0.0)
        nc.vector.memset(as_words(a_sc_first), 0)
        nc.vector.memset(as_words(b_sc_first), 0)
        nc.vector.memset(cap_rows[:], 0.0)
        make_identity(nc, ident[:])

        nc.scalar.dma_start(out=tb_col[0:2, :], in_=tau.rearrange("(r e) -> r e", e=2))
        nc.scalar.dma_start(out=tb_col[2:4, :], in_=bias.rearrange("(r e) -> r e", e=2))
        load_img(0, 0, 2)
        load_a(0)
        load_scales(a_sc_first, txt_d_scales, 0, 1)
        load_match(0, 0, 1)
        nc.sync.dma_start(out=cap_rows[0 : G * GROUPS, :], in_=cap_weight.rearrange("h (g k) -> (h g) k", k=K_PASS))
        load_img(0, 2, 4)
        load_match(0, 1, 2)
        load_img(1, 0, 4)
        load_match(0, 2, 3)
        load_scales(b_sc_first, txt_n_scales, 0, GROUPS)
        load_b(0)
        load_match(0, 3, 4)

        def load_later_shards():
            load_scales(a_sc_rest, txt_d_scales, 1, G)
            for h in range(1, G):
                load_a(h)
                load_match(h, 0, 2)
                if h + 1 < G:
                    load_img(h + 1, 0, 4)
                if h == 1:
                    load_scales(b_sc_rest, txt_n_scales, GROUPS, G * GROUPS)
                load_match(h, 2, 4)
                load_b(h)

        def a_scale(h, g):
            plane = a_sc_first[:, 0, :] if h == 0 else a_sc_rest[:, h - 1, :]
            return plane[:, K_PASS * g : K_PASS * (g + 1)]

        def b_scale(h, g):
            return b_sc_first[:, g, :] if h == 0 else b_sc_rest[:, GROUPS * (h - 1) + g, :]

        qin, codes, scales, s_banks, t_banks, diff, y_bank, y_bf, small = {}, {}, {}, {}, {}, {}, {}, {}, {}
        img_mx, sig_pool, diff_pool, s_tags, t_tags = {}, {}, {}, {}, {}
        free_s, free_t = list(S_TAGS), ["t0", "t1", "t2"]

        def valid(n):
            return 0 <= n < TILES

        def stage1(n, g, spare=None):
            h = n // TILES_PER_SHARD
            s_tags[n, g] = spare or free_s.pop(0)
            s_banks[n, g] = psum.tile([P, K_PASS], F32, name="s_bank", tag=s_tags[n, g])
            nc.tensor.matmul_mx(
                out=s_banks[n, g][:],
                lhsT=img_mx[n][0].bitcast(FP8X4),
                lhsT_scale=img_mx[n][1],
                rhs=a_words[h][:, 2 * K_PASS * g : 2 * K_PASS * (g + 1)].bitcast(FP4X4),
                rhs_scale=a_scale(h, g),
                start=True,
                stop=True,
            )

        def local(ap):
            return ap.rearrange("r t (q c) -> r q t c", c=4)

        def sigmoid(n, g):
            h = n // TILES_PER_SHARD
            if s_tags[n, g] in S_TAGS:
                free_s.append(s_tags[n, g])
            if n not in diff:
                diff[n] = work.tile([P, 4, 2 * P], F32, name="diff")
                sig_pool[n] = work.tile([P, 4, P], F32, name="sig_pool")
            dst = diff[n][:, :, P * g : P * (g + 1)] if g < 2 else sig_pool[n][:]
            nc.scalar.activation(
                out=local(dst),
                in_=s_banks[n, g][:].rearrange("r (q c t) -> r q t c", c=4, t=4),
                func=ACT.Sigmoid,
                bias=tb[:, 1, h : h + 1],
                scale=tb[:, 0, h : h + 1],
            )

        def subtract(n, lo, hi):
            part = local(diff[n][:, :, P * lo : P * hi])
            m = match_tile(n)[:, K_PASS * lo : K_PASS * hi].rearrange("r (q c t) -> r q t c", c=4, t=4)
            nc.vector.tensor_tensor(out=part, in0=part, in1=m, op=ALU.subtract)

        def subtract_pool(engine, n):
            host = sig_pool[n][:].rearrange("r t p -> r (t p)").bitcast(BF16) if n == 0 else match_tile(n)
            diff_pool[n] = host[:, 0 : 2 * K_PASS].bitcast(F32).rearrange("r (t p) -> r t p", t=4)
            m = match_tile(n)[:, 2 * K_PASS : 3 * K_PASS].rearrange("r (p t) -> r t p", t=4)
            engine.tensor_tensor(out=diff_pool[n], in0=sig_pool[n][:], in1=m, op=ALU.subtract)

        def turn_diff(n, g):
            t_tags[n, g] = free_t.pop(0)
            t_banks[n, g] = psum.tile([P, 4, P], F32, name="t_bank", tag=t_tags[n, g])
            for t in range(4):
                src = diff[n][:, t, P * g : P * (g + 1)] if g < 2 else diff_pool[n][:, t, :]
                nc.tensor.transpose(t_banks[n, g][:, t, :], src, ident[:])

        def weigh(n, g):
            free_t.append(t_tags[n, g])
            h = n // TILES_PER_SHARD
            nc.vector.tensor_tensor(
                out=qin[n][:, K_PASS * g : K_PASS * (g + 1)].rearrange("p (i t) -> p i t", t=4),
                in0=t_banks[n, g][:].rearrange("p t i -> p i t"),
                in1=cap_t[:, GROUPS * h + g, :].unsqueeze(1).to_broadcast([P, P, 4]),
                op=ALU.mult,
            )

        def turn_img(bank, slot, n):
            h, it = divmod(n, TILES_PER_SHARD)
            words = img_sb[h][:, it, :].bitcast(F32)
            for u in range(2):
                nc.tensor.transpose(bank[:, slot, u, :], words[:, u : 2 * P : 2], ident[:])

        def turn_y(bank, slot, n):
            words = y_bf[n][:].bitcast(F32)
            for u in range(2):
                nc.tensor.transpose(bank[:, slot, u, :], words[:, P * u : P * (u + 1)], ident[:])

        def small_bank(tag):
            return psum.tile([P, 2, 2, P], F32, name="small", tag=tag)

        def copy_words(copy, dst, bank, lo, hi):
            copy(
                out=dst.bitcast(F32).rearrange("p (w r u) -> p w r u", r=P, u=2),
                in_=bank[:, lo:hi, :, :].rearrange("p w u r -> p w r u"),
            )

        def turn_small(s):
            small[s] = small_bank("small")
            if valid(s + 6):
                turn_img(small[s], 0, s + 6)
            if valid(s - 3):
                turn_y(small[s], 1, s - 3)

        def copy_small(s):
            lo = 0 if valid(s + 6) else 1
            hi = 2 if valid(s - 3) else 1
            copy_words(nc.scalar.copy, qin[s + 1][:, IMG_AT + D * lo : IMG_AT + D * hi], small[s], lo, hi)

        def new_planes(s):
            codes[s] = work.tile([P, 4 * P], U32, name="codes", bufs=4, align_bytes=64)
            scales[s] = work.tile([P, 4 * P], U8, name="scales", bufs=4, align_bytes=64)

        def new_qin(s):
            qin[s] = work.tile([P, N + 2 * D], BF16, name="qin", bufs=5, align_bytes=64)

        def quantize(s, lo, hi):
            nc.vector.quantize_mx(
                out=codes[s][:, P * lo : P * hi].bitcast(FP8X4),
                scales=scales[s][:, P * lo : P * hi],
                in_=qin[s][:, K_PASS * lo : K_PASS * hi],
            )

        def slot(s, c):
            return codes[s][:, P * c : P * (c + 1)], scales[s][:, P * c : P * (c + 1)]

        def quantize_y(src, lo, hi):
            nc.vector.quantize_mx(
                out=y_codes[:, P * lo : P * hi].bitcast(FP8X4), scales=y_scales[:, P * lo : P * hi], in_=src
            )

        def stage2(n, tag, order=(0, 1, 2)):
            h = n // TILES_PER_SHARD
            y_bank[n] = psum.tile([P, D], F32, name="y_bank", tag=tag)
            for g in order:
                nc.tensor.matmul_mx(
                    out=y_bank[n][:],
                    lhsT=codes[n][:, P * g : P * (g + 1)].bitcast(FP8X4),
                    lhsT_scale=scales[n][:, P * g : P * (g + 1)],
                    rhs=b_words[h][:, g, :].bitcast(FP4X4),
                    rhs_scale=b_scale(h, g),
                    start=(g == order[0]),
                    stop=(g == order[-1]),
                )

        def store_y(n):
            h, it = divmod(n, TILES_PER_SHARD)
            nc.scalar.activation(out=y32[n][:], in_=y_bank[n][:], func=ACT.Copy, scale=tb[:, 0, h : h + 1])
            nc.sync.dma_start(out=out_0[h, P * it : P * (it + 1), :], in_=y32[n][:])

        def round_y(n):
            h = n // TILES_PER_SHARD
            y_bf[n] = work.tile([P, D], BF16, name="y_bf")
            nc.scalar.activation(
                out=y_bf[n][:].rearrange("r (u p e) -> r u p e", u=2, e=2),
                in_=y_bank[n][:].rearrange("r (p u e) -> r u p e", u=2, e=2),
                func=ACT.Copy,
                scale=tb[:, 0, h : h + 1],
            )

        words_out = out_1[0].rearrange("p m t -> p (m t)").bitcast(I32)
        scales_out = out_2[0].bitcast(I32)

        def store_codes(lo, hi):
            nc.sync.dma_start(out=words_out[:, P * lo : P * hi], in_=y_codes[:, P * lo : P * hi].bitcast(I32))

        def store_scales(lo, hi, queues):
            for q in range(4):
                queues[q % len(queues)].dma_start(
                    out=scales_out[4 * q : 4 * q + 4, P * lo // 4 : P * hi // 4],
                    in_=y_scales[32 * q : 32 * q + 4, P * lo : P * hi].bitcast(I32),
                )

        def turn_cap():
            bank = psum.tile([P, 4, P], F32, name="t_bank", tag="t1")
            words = cap_rows[:].bitcast(F32)
            for u in range(2):
                nc.tensor.transpose(bank[:, u, :], words[:, u : 2 * P : 2], ident[:])
            return bank

        def copy_cap(bank):
            nc.vector.tensor_copy(
                out=cap_t[:].bitcast(F32), in_=bank[:, 0:2, 0 : G * GROUPS].rearrange("p u c -> p c u")
            )

        last = TILES - 1

        new_qin(-1)
        new_planes(-1)
        for n in range(TILES_PER_SHARD):
            img_mx[n] = slot(-1, n)
        banks = [small_bank("t0"), small_bank("t1")]
        for n in range(2):
            turn_img(banks[n], 0, n)
        copy_words(nc.vector.tensor_copy, qin[-1][:, 0:D], banks[0], 0, 1)
        quantize(-1, 0, 1)
        copy_words(nc.vector.tensor_copy, qin[-1][:, D : 2 * D], banks[1], 0, 1)
        spread = psum.tile([P, P], F32, name="spread", tag="small")
        nc.tensor.transpose(spread[:], tb_col[:].bitcast(F32).to_broadcast([P, P]), ident[:])
        nc.vector.tensor_copy(out=tb[:].rearrange("p a h -> p (a h)"), in_=spread[:, 0:G].bitcast(BF16))
        nc.vector.memset(as_words(a_sc_rest), 0)
        quantize(-1, 1, 2)
        for g in range(GROUPS):
            stage1(0, g)
            sigmoid(0, g)
        bank = small_bank("t2")
        turn_img(bank, 0, 2)
        turn_img(bank, 1, 3)
        stage1(1, 0, "y")
        stage1(1, 1, "small")
        cap_bank = turn_cap()
        stage1(1, 2)
        for g in range(GROUPS):
            sigmoid(1, g)
        subtract(0, 0, 1)
        subtract(0, 1, 2)
        copy_words(nc.vector.tensor_copy, qin[-1][:, 2 * D : 4 * D], bank, 0, 2)
        subtract_pool(nc.vector, 0)
        copy_cap(cap_bank)
        quantize(-1, 2, 4)
        subtract(1, 0, 2)
        nc.gpsimd.memset(as_words(b_sc_rest), 0)
        load_later_shards()
        for g in range(GROUPS):
            turn_diff(0, g)
        new_qin(0)

        def quantize_early(s):
            new_planes(s)
            if not valid(s + 5):
                quantize(s, 0, 2)

        def quantize_late(s):
            if valid(s + 5):
                quantize(s, 0, 4)
                img_mx[s + 5] = slot(s, 3)
            else:
                quantize(s, 2, 3)

        def quantize_step_y(s):
            quantize_y(qin[s][:, Y_AT : Y_AT + D], s - 4, s - 3)

        for s in range(last):
            subtract_pool(nc.gpsimd, s + 1)
            if valid(s + 2):
                for g in (1, 0, 2):
                    stage1(s + 2, g)
                for g in range(GROUPS):
                    sigmoid(s + 2, g)
            if s == 0:
                bank = small_bank("y")
                turn_img(bank, 0, 4)
                turn_img(bank, 1, 5)
                copy_words(nc.scalar.copy, qin[-1][:, Y_AT : Y_AT + D], bank, 0, 1)
                copy_words(nc.scalar.copy, qin[0][:, IMG_AT : IMG_AT + D], bank, 1, 2)
            for g in (2, 0, 1):
                weigh(s, g)
            if valid(s - 2):
                stage2(s - 2, "y")
                store_y(s - 2)
                round_y(s - 2)
            turn_small(s)
            for g in range(GROUPS):
                turn_diff(s + 1, g)
            if valid(s - 5) and s < last - 1:
                quantize_step_y(s - 1)
                if s % TILES_PER_SHARD == 0:
                    store_codes(s - 8, s - 4)
                if s == last - 3:
                    store_scales(0, s - 4, [nc.sync])
            if s >= 1:
                quantize_early(s - 1)
            if valid(s + 2):
                subtract(s + 2, 0, 2)
            if s >= 1:
                quantize_late(s - 1)
            else:
                new_planes(-2)
                img_mx[4] = slot(-2, 0)
                nc.vector.quantize_mx(
                    out=img_mx[4][0].bitcast(FP8X4), scales=img_mx[4][1], in_=qin[-1][:, Y_AT : Y_AT + D]
                )
            new_qin(s + 1)
            copy_small(s)

        quantize_early(last - 1)
        quantize_late(last - 1)
        stage2(last - 2, "s0")
        round_y(last - 2)
        store_y(last - 2)
        stage2(last - 1, "y")
        pair = small_bank("s1")
        turn_y(pair, 0, last - 3)
        turn_y(pair, 1, last - 2)
        round_y(last - 1)
        store_y(last - 1)
        new_planes(last)
        weigh(last, 2)
        weigh(last, 0)
        quantize(last, 2, 3)
        weigh(last, 1)
        quantize(last, 0, 1)
        quantize(last, 1, 2)
        stage2(last, "s2", (2, 0, 1))
        round_y(last)
        new_qin(last + 1)
        rest = qin[last + 1]
        copy_words(nc.vector.tensor_copy, rest[:, 0 : 2 * D], pair, 0, 2)
        for s in range(last - 2, last + 1):
            quantize_step_y(s)
        store_codes(last - 7, last - 3)
        store_y(last)
        bank = small_bank("small")
        turn_y(bank, 0, last - 1)
        copy_words(nc.vector.tensor_copy, rest[:, 2 * D : 3 * D], bank, 0, 1)
        quantize_y(rest[:, 0 : 2 * D], last - 3, last - 1)
        quantize_y(rest[:, 2 * D : 3 * D], last - 1, last)
        bank = small_bank("s0")
        turn_y(bank, 0, last)
        copy_words(nc.vector.tensor_copy, rest[:, 3 * D : 4 * D], bank, 0, 1)
        quantize_y(rest[:, 3 * D : 4 * D], last, last + 1)
        store_codes(last - 3, last + 1)
        store_scales(last - 7, last + 1, [nc.scalar, nc.sync])
